import numpy as np
import ml_dtypes


def mxq(x, axis, fmt="e4m3"):
    dtype, down = {"e4m3": (ml_dtypes.float8_e4m3fn, 7), "e5m2": (ml_dtypes.float8_e5m2, 14)}[fmt]
    v = np.moveaxis(np.asarray(x, np.float32).astype(ml_dtypes.bfloat16).astype(np.float64), axis, -1)
    blocks = v.reshape(v.shape[:-1] + (-1, 32))
    amax = np.abs(blocks).max(-1, keepdims=True)
    byte = np.maximum(np.where(amax > 0, np.frexp(amax)[1] - 1 + 127, 0) - down, 1)
    scale = np.exp2(byte - 127.0)
    codes = (blocks / scale).astype(np.float32).astype(dtype).astype(np.float64)
    return np.moveaxis((codes * scale).reshape(v.shape), -1, axis)


WIDE = False


def mx_kscale(k):
    if not WIDE:
        return np.ones(k)
    levels = np.array([10, -10, 5, -5, 0])
    if k % 512:
        return np.exp2(np.random.permutation(np.resize(levels, k // 32))).repeat(32)
    a = np.empty((k // 512, 16))
    for p in range(k // 512):
        a[p, :8] = np.random.permutation(np.resize(levels, 8))
        for g in range(8):
            far = levels[np.abs(levels - a[p, g]) >= 10]
            a[p, g + 8] = far[np.random.randint(len(far))]
    return np.exp2(a.ravel()).repeat(32)


BF16 = ml_dtypes.bfloat16


def bf(x):
    return np.asarray(x, np.float32).astype(BF16)


def f64(x):
    return np.asarray(x).astype(np.float64)


E2M1 = np.array([0.0, 0.5, 1.0, 1.5, 2.0, 3.0, 4.0, 6.0, -0.0, -0.5, -1.0, -1.5, -2.0, -3.0, -4.0, -6.0])


def pack_weight(w, fmt):
    k, n = w.shape
    w = f64(bf(w)).reshape(k // 32, 32, n)
    amax = np.abs(w).max(1)
    if fmt == "e4m3":
        byte = np.frexp(amax)[1] - 1 + 127 - 7
    else:
        mant, ex = np.frexp(amax / 6.0)
        byte = np.where(mant > 0.5, ex, ex - 1) + 127
    byte = np.clip(np.where(amax > 0, byte, 1), 1, 254)
    scaled = (w * np.exp2(127.0 - byte)[:, None, :]).reshape(k, n).astype(np.float32)
    by_word = np.ascontiguousarray(scaled.reshape(k // 512, 128, 4, n).transpose(0, 1, 3, 2))
    if fmt == "e4m3":
        words = by_word.astype(ml_dtypes.float8_e4m3fn).view(np.uint8)
    else:
        c = by_word.astype(ml_dtypes.float4_e2m1fn).view(np.uint8) & 0xF
        words = c[..., 0::2] | (c[..., 1::2] << 4)
    return np.ascontiguousarray(words), np.ascontiguousarray(byte.astype(np.uint8).reshape(k // 512, 16, n))


def unpack_weight(words, scales, fmt):
    g, p, n, _ = words.shape
    if fmt == "e4m3":
        vals = np.ascontiguousarray(words).view(ml_dtypes.float8_e4m3fn).astype(np.float64)
    else:
        nib = np.empty((g, p, n, 4), np.uint8)
        nib[..., 0::2] = words & 0xF
        nib[..., 1::2] = words >> 4
        vals = E2M1[nib]
    vals = vals * np.repeat(np.exp2(scales.astype(np.float64) - 127.0), 8, axis=1)[..., None]
    return vals.transpose(0, 1, 3, 2).reshape(g * 512, n)
def pack4(w):
    words, scales = pack_weight(w, "e2m1")
    return words.reshape(words.shape[0], 128, -1), scales


def unpack4(words, scales):
    return unpack_weight(words.reshape(words.shape[0], 128, -1, 2), scales, "e2m1")


E4M3FN = np.array([(-1.0 if i & 128 else 1.0) * ((1.0 + (i & 7) / 8.0) * 2.0 ** (((i >> 3) & 15) - 7) if i & 120 else (i & 7) * 2.0 ** -9) for i in range(256)])


def e4m3fn_bytes(y):
    return np.clip(np.asarray(y, np.float64), -448.0, 448.0).astype(np.float32).astype(ml_dtypes.float8_e4m3fn).view(np.uint8)


def e4m3fn_values(b):
    return E4M3FN[b]


B, N, D, M, V = 2, 1024, 512, 512, 1024


def logsumexp(l, axis):
    m = l.max(axis=axis, keepdims=True)
    return m + np.log(np.sum(np.exp(l - m), axis=axis, keepdims=True))


def sinkhorn_round(l):
    n_tokens, n_slots = l.shape[1], l.shape[2]
    l = l - logsumexp(l, 2) + np.log(n_slots)
    l = l - logsumexp(l, 1) + np.log(n_tokens)
    return l


def draw0():
    s, t = mx_kscale(D), mx_kscale(N)
    x = np.random.standard_normal((B, N, D)) + 0.75 * np.random.standard_normal((1, 1, D))
    phi = (1.6 * np.random.standard_normal((D, M)) + 1.2 * np.random.standard_normal((D, 1))) / np.sqrt(D)
    w = 1.0 + 0.1 * np.random.standard_normal(N)
    v = np.random.standard_normal((B, N, V))
    words, scales = pack4(phi / s[:, None])
    return {"x": bf(x * s), "phi_words": words, "phi_scales": scales, "w": bf(w * t), "v": bf(v / t[:, None])}


def core(x, phi_words, phi_scales, w, v):
    n_tokens = x.shape[1]
    l = mxq(f64(x), 2, "e4m3") @ unpack4(phi_words, phi_scales)
    l = sinkhorn_round(l)
    l = sinkhorn_round(l)
    c = (np.exp(l) - 1.0) * f64(w)[None, :, None]
    cq = mxq(c, 1, "e4m3")
    vq = mxq(f64(v), 1, "e4m3")
    return (1.0 / np.sqrt(n_tokens)) * (np.swapaxes(cq, 1, 2) @ vq)


def setup_inputs():
    drawn = draw0()
    full = np.asarray(drawn['v']).astype(np.float64)
    scale = (np.abs(full).reshape(2, 8, 128, 8, 128).max(axis=(2, 4)) / 448.0).astype(np.float32)
    given = {}
    for key, value in drawn.items():
        if key == 'v':
            given['v_bytes'] = e4m3fn_bytes(full / np.repeat(np.repeat(scale.astype(np.float64), 128, axis=1), 128, axis=2))
            given['v_scale'] = scale
        else:
            given[key] = value
    return given


def reference(x, phi_words, phi_scales, w, v_bytes, v_scale):
    return core(x, phi_words, phi_scales, w, e4m3fn_values(v_bytes) * np.repeat(np.repeat(v_scale.astype(np.float64), 128, axis=1), 128, axis=2))

@@ -1,0 +1,370 @@
+from contextlib import ExitStack
+
+import concourse.mybir as mybir
+from concourse.masks import make_identity
+
+B, N, D, M, V = 2, 1024, 512, 512, 1024
+FLOPS = 2 * B * N * D * M + 2 * B * N * M * V
+
+P = 128
+MMB, TLB = 4, 2
+XTV = lambda b, j: b == 0 and j == 1
+PLV = lambda b, k: False
+OV = lambda b, j: b == 1 and j % 2 == 1
+VIS = lambda b, i: False
+LN2 = 0.6931471805599453
+F32 = mybir.dt.float32
+BF16 = mybir.dt.bfloat16
+I32 = mybir.dt.int32
+U32 = mybir.dt.uint32
+U8 = mybir.dt.uint8
+FP8 = mybir.dt.float8_e4m3fn
+FP8X4 = mybir.dt.float8_e4m3fn_x4
+FP4X4 = mybir.dt.float4_e2m1fn_x4
+ALU = mybir.AluOpType
+ACT = mybir.ActivationFunctionType
+X = mybir.AxisListType.X
+
+
+def tile_sinkhornbalancedslotdispatch_d2p_kernel(tc, x, phi_words, phi_scales, w, v_bytes, v_scale, out):
+    nc = tc.nc
+    with ExitStack() as ctx:
+        keep = ctx.enter_context(tc.tile_pool(name="keep", bufs=1))
+        work = ctx.enter_context(tc.tile_pool(name="work", bufs=2))
+        psum = ctx.enter_context(tc.psum_pool(name="psum", bufs=1))
+
+        ident = keep.tile([P, P], F32, name="ident")
+        make_identity(nc, ident[:])
+
+        phi_w = keep.tile([P, 2 * M], U8, name="phi_w", align_bytes=64)
+        phi_s = keep.tile([P, M], U8, name="phi_s", align_bytes=64)
+        nc.vector.memset(phi_s[:].bitcast(I32), 0)
+        for q in range(4):
+            nc.scalar.dma_start(out=phi_s[32 * q : 32 * q + 4, :].bitcast(I32), in_=phi_scales[0, 4 * q : 4 * q + 4, :].bitcast(I32))
+        nc.scalar.dma_start(out=phi_w[:].bitcast(I32), in_=phi_words[0].bitcast(I32))
+
+        x_sb = [[keep.tile([P, 4, D], BF16, name=f"x_{b}_{g}") for g in range(2)] for b in range(B)]
+        vb = [[keep.tile([P, 4, V], U8, name=f"vbytes_{b}_{g}") for g in range(2)] for b in range(B)]
+
+        def load_x(b, g):
+            nc.sync.dma_start(out=x_sb[b][g][:], in_=x[b].rearrange("(g p t) k -> g p t k", p=P, t=4)[g])
+
+        def load_v(b, g):
+            nc.sync.dma_start(out=vb[b][g][:], in_=v_bytes[b].rearrange("(g p t) j -> g p t j", p=P, t=4)[g])
+
+        load_x(0, 0)
+        load_x(0, 1)
+        load_v(0, 0)
+        load_x(1, 0)
+        load_x(1, 1)
+        load_v(0, 1)
+        load_v(1, 0)
+        load_v(1, 1)
+
+        w_bf = keep.tile([P, 2, 4], BF16, name="w_bf")
+        nc.gpsimd.dma_start(out=w_bf[:], in_=w.rearrange("(g p t) -> p g t", p=P, t=4))
+        vs = keep.tile([P, 4, 8], F32, name="vs")
+        vs_src = v_scale.rearrange("b i j -> (b i) j").rearrange("(c q) j -> q c j", q=4)
+        for q in range(4):
+            nc.gpsimd.dma_start(out=vs[32 * q : 32 * q + 32], in_=vs_src[q].partition_broadcast(32))
+
+        w32 = keep.tile([P, 8], F32, name="w32")
+
+        xc = [[keep.tile([P, 512], U32, name=f"xc_{b}_{g}", align_bytes=64) for g in range(2)] for b in range(B)]
+        xs = [[keep.tile([P, 512], U8, name=f"xs_{b}_{g}", align_bytes=64) for g in range(2)] for b in range(B)]
+        cq = [[keep.tile([P, 512], U32, name=f"cq_{b}_{g}", align_bytes=64) for g in range(2)] for b in range(B)]
+        cs = [[keep.tile([P, 512], U8, name=f"cs_{b}_{g}", align_bytes=64) for g in range(2)] for b in range(B)]
+        vq = [[keep.tile([P, V], U32, name=f"vq_{b}_{g}", align_bytes=64) for g in range(2)] for b in range(B)]
+        vqs = [[keep.tile([P, V], U8, name=f"vqs_{b}_{g}", align_bytes=64) for g in range(2)] for b in range(B)]
+        nl = [keep.tile([P, 8, M], F32, name=f"nl_{b}") for b in range(B)]
+        et = [keep.tile([P, 4, N], F32, name=f"et_{b}") for b in range(B)]
+        na = [keep.tile([P, 8], F32, name=f"na_{b}") for b in range(B)]
+        r1 = [keep.tile([P, 8], F32, name=f"r1_{b}") for b in range(B)]
+        lnr = [keep.tile([P, 8], F32, name=f"lnr_{b}") for b in range(B)]
+        lnt = [keep.tile([P, 8], F32, name=f"lnt_{b}") for b in range(B)]
+        lse = [keep.tile([P, 8], F32, name=f"lse_{b}") for b in range(B)]
+        nb2 = [keep.tile([P, 4, 2], F32, name=f"nb2_{b}") for b in range(B)]
+        nb = [keep.tile([P, 4], F32, name=f"nb_{b}") for b in range(B)]
+        s1 = [keep.tile([P, 4, 2], F32, name=f"s1_{b}") for b in range(B)]
+        s1t = [keep.tile([P, 4], F32, name=f"s1t_{b}") for b in range(B)]
+        v1 = [keep.tile([P, 4], F32, name=f"v1_{b}") for b in range(B)]
+        s2 = [keep.tile([P, 4], F32, name=f"s2_{b}") for b in range(B)]
+        usb = [keep.tile([P, N], F32, name=f"usb_{b}") for b in range(B)]
+        r2 = [keep.tile([P, 8], F32, name=f"r2_{b}") for b in range(B)]
+        u2 = [keep.tile([P, 8], F32, name=f"u2_{b}") for b in range(B)]
+        v2 = [keep.tile([P, 4], F32, name=f"v2_{b}") for b in range(B)]
+
+        xt_ps = {}
+        o_ps = {}
+        xg = {}
+        wide = {}
+        vg = {}
+        cc = {}
+        cgs = {}
+        slot_ps = {}
+        r2_ps = {}
+        l_ps = {}
+
+        def xt_pe(b, j):
+            g, h = divmod(j, 2)
+            ps = psum.tile([P, 2, 2, P], F32, name="xt_ps", tag="mm", bufs=MMB)
+            words = x_sb[b][g][:].bitcast(F32)
+            for k in range(2):
+                for e in range(2):
+                    nc.tensor.transpose(ps[:, k, e, :], words[:, 2 * h + k, e:256:2], ident[:])
+            xt_ps[b, j] = ps
+
+        def xt_cp(b, j):
+            g, h = divmod(j, 2)
+            if (b, g) not in xg:
+                xg[b, g] = work.tile([P, 512, 4], BF16, name="xg", tag="xg", bufs=2, align_bytes=64)
+            dst = xg[b, g][:].bitcast(F32)[:, 256 * h : 256 * h + 256, :].rearrange("p (k r) e -> p k r e", k=2)
+            src = xt_ps[b, j][:].rearrange("p k e r -> p k r e")
+            if XTV(b, j):
+                nc.vector.tensor_copy(out=dst, in_=src)
+            else:
+                nc.scalar.copy(out=dst, in_=src)
+
+        def qx(b, g):
+            nc.vector.quantize_mx(out=xc[b][g][:].bitcast(FP8X4), scales=xs[b][g][:], in_=xg[b, g][:].rearrange("p r k -> p (r k)"))
+
+        def mx1(b, i):
+            g, t = i // 4, i % 4
+            ps = psum.tile([P, M], F32, name="l_ps", tag="mm", bufs=MMB)
+            nc.tensor.matmul_mx(
+                out=ps[:],
+                lhsT=xc[b][g][:, P * t : P * t + P].bitcast(FP8X4),
+                lhsT_scale=xs[b][g][:, P * t : P * t + P],
+                rhs=phi_w[:].bitcast(FP4X4),
+                rhs_scale=phi_s[:],
+                start=True,
+                stop=True,
+            )
+            l_ps[b, i] = ps
+
+        def row_v(b, i):
+            nc.vector.tensor_scalar(out=nl[b][:, i, :], in0=l_ps[b, i][:], scalar1=-1.0, scalar2=None, op0=ALU.mult, op1=ALU.min, accum_out=na[b][:, i : i + 1])
+
+        def row_s(b, i):
+            junk = work.tile([P, M], BF16, name="junk", tag="junk", bufs=2)
+            nc.scalar.activation(out=junk[:], in_=nl[b][:, i, :], func=ACT.Exp, scale=-1.0, bias=na[b][:, i : i + 1], accum_out=r1[b][:, i : i + 1])
+
+        def ln_a(b, n):
+            if n == 0:
+                nc.vector.tensor_copy(out=lnt[b][:], in_=r1[b][:].bitcast(I32))
+            else:
+                nc.vector.tensor_tensor(out=lnt[b][:], in0=lnt[b][:], in1=r1[b][:], op=ALU.mult)
+
+        def ln_b(b, n):
+            y, f = lnr[b][:], lnt[b][:]
+            if n == 0:
+                nc.vector.tensor_scalar(out=y, in0=f, scalar1=LN2 / 2**23, scalar2=-126.957 * LN2, op0=ALU.mult, op1=ALU.add)
+            else:
+                nc.vector.scalar_tensor_tensor(out=y, in0=f, scalar=-1.0, in1=y, op0=ALU.add, op1=ALU.add)
+
+        def ln_c(b, n):
+            nc.vector.tensor_tensor(out=lse[b][:], in0=lnr[b][:], in1=na[b][:], op=ALU.subtract)
+
+        def ln_s(b, n):
+            nc.scalar.activation(out=lnt[b][:], in_=lnr[b][:], func=ACT.Exp, scale=-1.0)
+
+        def col_pe(b, j):
+            k, g = divmod(j, 2)
+            ps = psum.tile([P, 4, P], F32, name="t_ps", tag="tl", bufs=TLB)
+            for t in range(4):
+                i = 4 * g + t
+                nc.tensor.matmul(ps[:, t, :], lhsT=nl[b][:, i, P * k : P * k + P], rhs=ident[:], is_transpose=True, start=True, stop=False)
+                nc.tensor.matmul(ps[:, t, :], lhsT=lse[b][:, i : i + 1].to_broadcast([P, P]), rhs=ident[:], is_transpose=True, start=False, stop=True)
+            slot_ps[b, k, g] = ps
+
+        def col_max(b, j):
+            k, g = divmod(j, 2)
+            nc.vector.tensor_reduce(out=nb2[b][:, k, g : g + 1], in_=slot_ps[b, k, g][:].rearrange("p t r -> p (t r)"), axis=X, op=ALU.min)
+
+        def col_min2(b, k):
+            nc.vector.tensor_tensor(out=nb[b][:, k : k + 1], in0=nb2[b][:, k, 0:1], in1=nb2[b][:, k, 1:2], op=ALU.min)
+
+        def col_exp(b, j):
+            k, g = divmod(j, 2)
+            nc.scalar.activation(
+                out=et[b][:, k, 512 * g : 512 * g + 512],
+                in_=slot_ps[b, k, g][:].rearrange("p t r -> p (t r)"),
+                func=ACT.Exp,
+                scale=-1.0,
+                bias=nb[b][:, k : k + 1],
+                accum_out=s1[b][:, k, g : g + 1],
+            )
+
+        def col_add(b, k):
+            nc.vector.tensor_tensor(out=s1t[b][:, k : k + 1], in0=s1[b][:, k, 0:1], in1=s1[b][:, k, 1:2], op=ALU.add)
+
+        def col_rcp(b, k):
+            nc.vector.reciprocal(out=v1[b][:, k : k + 1], in_=s1t[b][:, k : k + 1])
+
+        def row2_scale(b, k):
+            nc.scalar.activation(out=et[b][:, k, :], in_=et[b][:, k, :], func=ACT.Copy, scale=v1[b][:, k : k + 1])
+
+        def row2_pe(b, g):
+            ps = psum.tile([P, 4, P], F32, name="r2_ps", tag="tl", bufs=TLB)
+            for t in range(4):
+                i = 4 * g + t
+                for k in range(4):
+                    nc.tensor.matmul(ps[:, t, :], lhsT=et[b][:, k, P * i : P * i + P], rhs=ident[:], is_transpose=True, start=(k == 0), stop=(k == 3))
+            r2_ps[b, g] = ps
+
+        def row2_sum(b, g):
+            nc.vector.tensor_reduce(out=r2[b][:, 4 * g : 4 * g + 4], in_=r2_ps[b, g][:], axis=X, op=ALU.add)
+
+        def row2_rcp(b, g):
+            nc.vector.reciprocal(out=u2[b][:, 4 * g : 4 * g + 4], in_=r2[b][:, 4 * g : 4 * g + 4])
+
+        ubc = {}
+
+        def row2_bc(b, g):
+            ps = psum.tile([P, 4, P], F32, name="u_ps", tag="u", bufs=2)
+            for t in range(4):
+                i = 4 * g + t
+                nc.tensor.matmul(ps[:, t, :], lhsT=u2[b][:, i : i + 1].to_broadcast([P, P]), rhs=ident[:], is_transpose=True, start=True, stop=True)
+            ubc[b, g] = ps
+
+        def row2_cp(b, g):
+            nc.scalar.copy(out=usb[b][:, 512 * g : 512 * g + 512], in_=ubc[b, g][:].rearrange("p t r -> p (t r)"))
+
+        def col2(b, k):
+            e = et[b][:, k, :]
+            nc.vector.scalar_tensor_tensor(out=e, in0=e, scalar=1.0, in1=usb[b][:], op0=ALU.mult, op1=ALU.mult, accum_out=s2[b][:, k : k + 1])
+
+        def col2_v(b, k):
+            nc.vector.reciprocal(out=v2[b][:, k : k + 1], in_=s2[b][:, k : k + 1])
+
+        def plan(b, k):
+            e = et[b][:, k, :]
+            if PLV(b, k):
+                nc.vector.tensor_scalar(out=e, in0=e, scalar1=v2[b][:, k : k + 1], scalar2=-1.0 / N, op0=ALU.mult, op1=ALU.add)
+            else:
+                nc.scalar.activation(out=e, in_=e, func=ACT.Identity, scale=v2[b][:, k : k + 1], bias=-1.0 / N)
+
+        tok_ps = {}
+        cg = {}
+
+        def tok_pe(b, j):
+            k, g = divmod(j, 2)
+            ps = psum.tile([P, 4, P], F32, name="tok_ps", tag="mm", bufs=MMB)
+            for t in range(4):
+                i = 4 * g + t
+                nc.tensor.transpose(ps[:, t, :], et[b][:, k, P * i : P * i + P], ident[:])
+            tok_ps[b, j] = ps
+
+        def coeff(b, j):
+            k, g = divmod(j, 2)
+            cg[b, j] = work.tile([P, P, 4], BF16, name="cg", tag="cg", bufs=3, align_bytes=64)
+            nc.vector.tensor_tensor(
+                out=cg[b, j][:],
+                in0=tok_ps[b, j][:].rearrange("p t m -> p m t"),
+                in1=w32[:, 4 * g : 4 * g + 4].unsqueeze(1).to_broadcast([P, P, 4]),
+                op=ALU.mult,
+            )
+
+        def c_quant(b, j):
+            k, g = divmod(j, 2)
+            nc.vector.quantize_mx(out=cq[b][g][:, P * k : P * k + P].bitcast(FP8X4), scales=cs[b][g][:, P * k : P * k + P], in_=cg[b, j][:].rearrange("p m t -> p (m t)"))
+
+        def widen(b, j):
+            g, t = divmod(j, 4)
+            if (b, g) not in wide:
+                wide[b, g] = work.tile([P, 4, V], BF16, name="wide", tag="wide", bufs=2)
+            nc.scalar.copy(out=wide[b, g][:, t, :], in_=vb[b][g][:, t, :].bitcast(FP8))
+
+        def v_ilv(b, i):
+            g, j = divmod(i, 8)
+            if (b, g) not in vg:
+                vg[b, g] = work.tile([P, V, 4], BF16, name="vg", tag="vg", bufs=2, align_bytes=64)
+            dst = vg[b, g][:, P * j : P * j + P, :]
+            src = wide[b, g][:, :, P * j : P * j + P].rearrange("p t j -> p j t")
+            if VIS(b, i):
+                nc.scalar.activation(out=dst, in_=src, func=ACT.Copy, scale=vs[:, 2 * b + g, j : j + 1])
+            else:
+                nc.vector.tensor_scalar(out=dst, in0=src, scalar1=vs[:, 2 * b + g, j : j + 1], scalar2=None, op0=ALU.mult)
+
+        def v_quant(b, g):
+            nc.vector.quantize_mx(out=vq[b][g][:].bitcast(FP8X4), scales=vqs[b][g][:], in_=vg[b, g][:].rearrange("p j t -> p (j t)"))
+
+        def o_pe(b, j):
+            mb, jh = divmod(j, 2)
+            ps = psum.tile([P, 512], F32, name="o_ps", tag="mm", bufs=MMB)
+            for g in range(2):
+                nc.tensor.matmul_mx(
+                    out=ps[:],
+                    lhsT=cq[b][g][:, P * mb : P * mb + P].bitcast(FP8X4),
+                    lhsT_scale=cs[b][g][:, P * mb : P * mb + P],
+                    rhs=vq[b][g][:, 512 * jh : 512 * jh + 512].bitcast(FP8X4),
+                    rhs_scale=vqs[b][g][:, 512 * jh : 512 * jh + 512],
+                    start=(g == 0),
+                    stop=(g == 1),
+                )
+            o_ps[b, j] = ps
+
+        def o_cp(b, j):
+            mb, jh = divmod(j, 2)
+            ot = work.tile([P, 512], F32, name="ot", tag="ot", bufs=8)
+            if OV(b, j):
+                nc.vector.tensor_scalar(out=ot[:], in0=o_ps[b, j][:], scalar1=1.0 / 32.0, scalar2=None, op0=ALU.mult)
+            else:
+                nc.scalar.activation(out=ot[:], in_=o_ps[b, j][:], func=ACT.Copy, scale=1.0 / 32.0)
+            nc.sync.dma_start(out=out[b, P * mb : P * mb + P, 512 * jh : 512 * jh + 512], in_=ot[:])
+
+        def prep_w(b, j):
+            nc.vector.tensor_scalar(out=w32[:], in0=w_bf[:].rearrange("p g t -> p (g t)"), scalar1=float(N), scalar2=None, op0=ALU.mult)
+
+        byname = {"xt_pe": xt_pe, "xt_cp": xt_cp, "qx": qx, "mx1": mx1, "row_v": row_v, "row_s": row_s, "ln_a": ln_a, "ln_b": ln_b, "ln_s": ln_s, "ln_c": ln_c, "prep_w": prep_w, "col_pe": col_pe, "col_max": col_max, "col_min2": col_min2, "col_exp": col_exp, "col_add": col_add, "col_rcp": col_rcp, "row2_scale": row2_scale, "row2_pe": row2_pe, "row2_sum": row2_sum, "row2_rcp": row2_rcp, "row2_bc": row2_bc, "row2_cp": row2_cp, "col2": col2, "col2_v": col2_v, "plan": plan, "tok_pe": tok_pe, "coeff": coeff, "c_quant": c_quant, "widen": widen, "v_ilv": v_ilv, "v_quant": v_quant, "o_pe": o_pe, "o_cp": o_cp}
+        table = (
+            "xt_pe.0.0 xt_pe.0.1 xt_cp.0.0 xt_pe.0.2 xt_cp.0.1 xt_pe.0.3 xt_cp.0.2 qx.0.0 "
+            "xt_pe.1.0 xt_cp.0.3 prep_w.0.0 xt_pe.1.1 xt_cp.1.0 qx.0.1 mx1.0.0 mx1.0.1 "
+            "xt_cp.1.1 row_v.0.0 mx1.0.2 widen.0.0 mx1.0.3 row_v.0.1 mx1.0.4 row_s.0.0 "
+            "row_v.0.2 mx1.0.5 row_s.0.1 row_v.0.3 mx1.0.6 row_s.0.2 row_v.0.4 widen.0.1 "
+            "mx1.0.7 row_v.0.5 row_s.0.3 xt_pe.1.2 row_v.0.6 row_s.0.4 xt_pe.1.3 row_v.0.7 "
+            "row_s.0.5 qx.1.0 row_s.0.6 row_s.0.7 mx1.1.0 mx1.1.1 xt_cp.1.2 row_v.1.0 "
+            "xt_cp.1.3 ln_a.0.0 row_v.1.1 mx1.1.2 mx1.1.3 row_s.1.0 ln_b.0.0 qx.1.1 "
+            "ln_s.0.1 row_s.1.1 row_v.1.2 mx1.1.4 widen.0.2 mx1.1.5 ln_a.0.1 row_v.1.3 "
+            "mx1.1.6 row_s.1.2 ln_b.0.1 row_v.1.4 mx1.1.7 row_s.1.3 row_v.1.5 ln_s.0.2 "
+            "row_s.1.4 ln_a.0.2 row_v.1.6 widen.0.3 ln_b.0.2 row_s.1.5 row_v.1.7 ln_s.0.3 "
+            "row_s.1.6 v_ilv.0.0 ln_a.0.3 v_ilv.0.1 row_s.1.7 ln_b.0.3 v_ilv.0.2 widen.0.4 "
+            "ln_c.0.0 v_ilv.0.3 col_pe.0.0 ln_a.1.0 v_ilv.0.4 widen.0.5 ln_b.1.0 v_ilv.0.5 "
+            "col_pe.0.1 ln_s.1.1 widen.0.6 col_max.0.0 widen.0.7 ln_a.1.1 v_ilv.0.6 col_max.0.1 "
+            "ln_b.1.1 v_ilv.0.7 ln_s.1.2 col_min2.0.0 v_ilv.0.8 widen.1.0 ln_a.1.2 v_ilv.0.9 "
+            "col_exp.0.0 ln_b.1.2 v_ilv.0.10 v_ilv.0.11 col_exp.0.1 v_ilv.0.12 col_pe.0.2 v_ilv.0.13 "
+            "ln_s.1.3 widen.1.1 col_add.0.0 ln_a.1.3 col_pe.0.3 v_ilv.0.14 widen.1.2 col_rcp.0.0 "
+            "col_max.0.2 row2_scale.0.0 col_max.0.3 ln_b.1.3 v_ilv.0.15 widen.1.3 col_min2.0.1 ln_c.1.0 "
+            "v_quant.0.0 col_exp.0.2 col_exp.0.3 v_quant.0.1 col_pe.0.4 widen.1.4 col_pe.0.5 widen.1.5 "
+            "col_max.0.4 widen.1.6 col_max.0.5 widen.1.7 col_add.0.1 v_ilv.1.0 col_min2.0.2 col_rcp.0.1 "
+            "v_ilv.1.1 col_exp.0.4 v_ilv.1.2 v_ilv.1.3 col_exp.0.5 col_pe.0.6 v_ilv.1.4 row2_scale.0.1 "
+            "v_ilv.1.5 col_pe.0.7 col_add.0.2 v_ilv.1.6 col_rcp.0.2 col_max.0.6 row2_scale.0.2 col_max.0.7 "
+            "v_ilv.1.7 col_min2.0.3 v_ilv.1.8 col_exp.0.6 v_ilv.1.9 v_ilv.1.10 col_exp.0.7 v_ilv.1.11 "
+            "col_pe.1.0 v_ilv.1.12 col_add.0.3 col_pe.1.1 v_ilv.1.13 col_rcp.0.3 col_max.1.0 row2_scale.0.3 "
+            "col_max.1.1 v_ilv.1.14 col_min2.1.0 v_ilv.1.15 col_exp.1.0 v_quant.1.0 col_exp.1.1 row2_pe.0.0 "
+            "v_quant.1.1 row2_pe.0.1 col_add.1.0 row2_sum.0.0 col_rcp.1.0 row2_rcp.0.0 row2_scale.1.0 row2_bc.0.0 "
+            "row2_sum.0.1 col_pe.1.2 row2_cp.0.0 row2_rcp.0.1 col_pe.1.3 col_max.1.2 row2_bc.0.1 col_max.1.3 "
+            "row2_cp.0.1 col_min2.1.1 col_exp.1.2 col2.0.0 col_exp.1.3 col_pe.1.4 col2.0.1 col_pe.1.5 "
+            "col_max.1.4 col_max.1.5 col2_v.0.0 col2_v.0.1 col_add.1.1 col_min2.1.2 plan.0.0 col2.0.2 "
+            "col_exp.1.4 col_rcp.1.1 col2.0.3 tok_pe.0.0 tok_pe.0.1 col_exp.1.5 col_pe.1.6 row2_scale.1.1 "
+            "coeff.0.0 col_pe.1.7 col_max.1.6 plan.0.1 coeff.0.1 col_max.1.7 col2_v.0.2 col2_v.0.3 "
+            "tok_pe.0.2 col_add.1.2 col_min2.1.3 plan.0.2 c_quant.0.0 c_quant.0.1 tok_pe.0.3 col_rcp.1.2 "
+            "coeff.0.2 o_pe.0.0 coeff.0.3 col_exp.1.6 o_pe.0.1 c_quant.0.2 c_quant.0.3 tok_pe.0.4 "
+            "col_exp.1.7 o_pe.0.2 coeff.0.4 row2_scale.1.2 col_add.1.3 c_quant.0.4 o_pe.0.3 col_rcp.1.3 "
+            "row2_scale.1.3 o_cp.0.0 row2_pe.1.0 o_cp.0.1 o_cp.0.2 row2_pe.1.1 o_cp.0.3 row2_sum.1.0 "
+            "plan.0.3 row2_rcp.1.0 row2_bc.1.0 row2_sum.1.1 tok_pe.0.5 row2_cp.1.0 tok_pe.0.6 coeff.0.5 "
+            "tok_pe.0.7 row2_rcp.1.1 coeff.0.6 row2_bc.1.1 coeff.0.7 row2_cp.1.1 c_quant.0.5 c_quant.0.6 "
+            "c_quant.0.7 o_pe.0.4 col2.1.0 o_pe.0.5 o_cp.0.4 o_pe.0.6 col2.1.1 o_cp.0.5 "
+            "o_pe.0.7 o_cp.0.6 col2_v.1.0 o_cp.0.7 col2.1.2 plan.1.0 col2_v.1.1 col2.1.3 "
+            "plan.1.1 tok_pe.1.0 tok_pe.1.1 col2_v.1.2 coeff.1.0 plan.1.2 tok_pe.1.2 col2_v.1.3 "
+            "coeff.1.1 tok_pe.1.3 c_quant.1.0 coeff.1.2 plan.1.3 tok_pe.1.4 c_quant.1.1 tok_pe.1.5 "
+            "coeff.1.3 o_pe.1.0 c_quant.1.2 coeff.1.4 tok_pe.1.6 o_cp.1.0 c_quant.1.3 coeff.1.5 "
+            "tok_pe.1.7 c_quant.1.4 coeff.1.6 o_pe.1.2 c_quant.1.5 coeff.1.7 o_cp.1.2 o_pe.1.1 "
+            "c_quant.1.6 o_cp.1.1 o_pe.1.4 c_quant.1.7 o_pe.1.3 o_cp.1.4 o_cp.1.3 o_pe.1.6 "
+            "o_pe.1.5 o_cp.1.6 o_cp.1.5 o_pe.1.7 o_cp.1.7 "
+        )
+        with tc.manual_schedule():
+            for word in table.split(" "):
+                if word:
+                    name, b, j = word.split(".")
+                    byname[name](int(b), int(j))

@@ -7,11 +7,12 @@ B, N, D, M, V = 2, 1024, 512, 512, 1024
 FLOPS = 2 * B * N * D * M + 2 * B * N * M * V
 
 P = 128
-MMB, TLB = 4, 2
+MMB, TLB = 4, 4
 XTV = lambda b, j: b == 0 and j == 1
 PLV = lambda b, k: False
-OV = lambda b, j: b == 1 and j % 2 == 1
-VIS = lambda b, i: False
+OV = lambda b, j: b == 1 and j in (5, 7)
+VIS = lambda b, i: i % 4 == 3
+WG = lambda b, j: True
 LN2 = 0.6931471805599453
 F32 = mybir.dt.float32
 BF16 = mybir.dt.bfloat16
@@ -221,7 +222,7 @@ def tile_sinkhornbalancedslotdispatch_d2p_kernel(tc, x, phi_words, phi_scales, w
         ubc = {}
 
         def row2_bc(b, g):
-            ps = psum.tile([P, 4, P], F32, name="u_ps", tag="u", bufs=2)
+            ps = psum.tile([P, 4, P], F32, name="u_ps", tag="mm", bufs=MMB)
             for t in range(4):
                 i = 4 * g + t
                 nc.tensor.matmul(ps[:, t, :], lhsT=u2[b][:, i : i + 1].to_broadcast([P, P]), rhs=ident[:], is_transpose=True, start=True, stop=True)
@@ -273,7 +274,11 @@ def tile_sinkhornbalancedslotdispatch_d2p_kernel(tc, x, phi_words, phi_scales, w
             g, t = divmod(j, 4)
             if (b, g) not in wide:
                 wide[b, g] = work.tile([P, 4, V], BF16, name="wide", tag="wide", bufs=2)
-            nc.scalar.copy(out=wide[b, g][:, t, :], in_=vb[b][g][:, t, :].bitcast(FP8))
+            src = vb[b][g][:, t, :].bitcast(FP8)
+            if WG(b, j):
+                nc.gpsimd.tensor_copy(out=wide[b, g][:, t, :], in_=src)
+            else:
+                nc.scalar.copy(out=wide[b, g][:, t, :], in_=src)
 
         def v_ilv(b, i):
             g, j = divmod(i, 8)
@@ -320,48 +325,48 @@ def tile_sinkhornbalancedslotdispatch_d2p_kernel(tc, x, phi_words, phi_scales, w
         table = (
             "xt_pe.0.0 xt_pe.0.1 xt_cp.0.0 xt_pe.0.2 xt_cp.0.1 xt_pe.0.3 xt_cp.0.2 qx.0.0 "
             "xt_pe.1.0 xt_cp.0.3 prep_w.0.0 xt_pe.1.1 xt_cp.1.0 qx.0.1 mx1.0.0 mx1.0.1 "
-            "xt_cp.1.1 row_v.0.0 mx1.0.2 widen.0.0 mx1.0.3 row_v.0.1 mx1.0.4 row_s.0.0 "
-            "row_v.0.2 mx1.0.5 row_s.0.1 row_v.0.3 mx1.0.6 row_s.0.2 row_v.0.4 widen.0.1 "
-            "mx1.0.7 row_v.0.5 row_s.0.3 xt_pe.1.2 row_v.0.6 row_s.0.4 xt_pe.1.3 row_v.0.7 "
-            "row_s.0.5 qx.1.0 row_s.0.6 row_s.0.7 mx1.1.0 mx1.1.1 xt_cp.1.2 row_v.1.0 "
-            "xt_cp.1.3 ln_a.0.0 row_v.1.1 mx1.1.2 mx1.1.3 row_s.1.0 ln_b.0.0 qx.1.1 "
-            "ln_s.0.1 row_s.1.1 row_v.1.2 mx1.1.4 widen.0.2 mx1.1.5 ln_a.0.1 row_v.1.3 "
-            "mx1.1.6 row_s.1.2 ln_b.0.1 row_v.1.4 mx1.1.7 row_s.1.3 row_v.1.5 ln_s.0.2 "
-            "row_s.1.4 ln_a.0.2 row_v.1.6 widen.0.3 ln_b.0.2 row_s.1.5 row_v.1.7 ln_s.0.3 "
-            "row_s.1.6 v_ilv.0.0 ln_a.0.3 v_ilv.0.1 row_s.1.7 ln_b.0.3 v_ilv.0.2 widen.0.4 "
-            "ln_c.0.0 v_ilv.0.3 col_pe.0.0 ln_a.1.0 v_ilv.0.4 widen.0.5 ln_b.1.0 v_ilv.0.5 "
-            "col_pe.0.1 ln_s.1.1 widen.0.6 col_max.0.0 widen.0.7 ln_a.1.1 v_ilv.0.6 col_max.0.1 "
-            "ln_b.1.1 v_ilv.0.7 ln_s.1.2 col_min2.0.0 v_ilv.0.8 widen.1.0 ln_a.1.2 v_ilv.0.9 "
-            "col_exp.0.0 ln_b.1.2 v_ilv.0.10 v_ilv.0.11 col_exp.0.1 v_ilv.0.12 col_pe.0.2 v_ilv.0.13 "
-            "ln_s.1.3 widen.1.1 col_add.0.0 ln_a.1.3 col_pe.0.3 v_ilv.0.14 widen.1.2 col_rcp.0.0 "
-            "col_max.0.2 row2_scale.0.0 col_max.0.3 ln_b.1.3 v_ilv.0.15 widen.1.3 col_min2.0.1 ln_c.1.0 "
-            "v_quant.0.0 col_exp.0.2 col_exp.0.3 v_quant.0.1 col_pe.0.4 widen.1.4 col_pe.0.5 widen.1.5 "
-            "col_max.0.4 widen.1.6 col_max.0.5 widen.1.7 col_add.0.1 v_ilv.1.0 col_min2.0.2 col_rcp.0.1 "
-            "v_ilv.1.1 col_exp.0.4 v_ilv.1.2 v_ilv.1.3 col_exp.0.5 col_pe.0.6 v_ilv.1.4 row2_scale.0.1 "
-            "v_ilv.1.5 col_pe.0.7 col_add.0.2 v_ilv.1.6 col_rcp.0.2 col_max.0.6 row2_scale.0.2 col_max.0.7 "
-            "v_ilv.1.7 col_min2.0.3 v_ilv.1.8 col_exp.0.6 v_ilv.1.9 v_ilv.1.10 col_exp.0.7 v_ilv.1.11 "
-            "col_pe.1.0 v_ilv.1.12 col_add.0.3 col_pe.1.1 v_ilv.1.13 col_rcp.0.3 col_max.1.0 row2_scale.0.3 "
-            "col_max.1.1 v_ilv.1.14 col_min2.1.0 v_ilv.1.15 col_exp.1.0 v_quant.1.0 col_exp.1.1 row2_pe.0.0 "
-            "v_quant.1.1 row2_pe.0.1 col_add.1.0 row2_sum.0.0 col_rcp.1.0 row2_rcp.0.0 row2_scale.1.0 row2_bc.0.0 "
-            "row2_sum.0.1 col_pe.1.2 row2_cp.0.0 row2_rcp.0.1 col_pe.1.3 col_max.1.2 row2_bc.0.1 col_max.1.3 "
-            "row2_cp.0.1 col_min2.1.1 col_exp.1.2 col2.0.0 col_exp.1.3 col_pe.1.4 col2.0.1 col_pe.1.5 "
-            "col_max.1.4 col_max.1.5 col2_v.0.0 col2_v.0.1 col_add.1.1 col_min2.1.2 plan.0.0 col2.0.2 "
-            "col_exp.1.4 col_rcp.1.1 col2.0.3 tok_pe.0.0 tok_pe.0.1 col_exp.1.5 col_pe.1.6 row2_scale.1.1 "
-            "coeff.0.0 col_pe.1.7 col_max.1.6 plan.0.1 coeff.0.1 col_max.1.7 col2_v.0.2 col2_v.0.3 "
-            "tok_pe.0.2 col_add.1.2 col_min2.1.3 plan.0.2 c_quant.0.0 c_quant.0.1 tok_pe.0.3 col_rcp.1.2 "
-            "coeff.0.2 o_pe.0.0 coeff.0.3 col_exp.1.6 o_pe.0.1 c_quant.0.2 c_quant.0.3 tok_pe.0.4 "
-            "col_exp.1.7 o_pe.0.2 coeff.0.4 row2_scale.1.2 col_add.1.3 c_quant.0.4 o_pe.0.3 col_rcp.1.3 "
-            "row2_scale.1.3 o_cp.0.0 row2_pe.1.0 o_cp.0.1 o_cp.0.2 row2_pe.1.1 o_cp.0.3 row2_sum.1.0 "
-            "plan.0.3 row2_rcp.1.0 row2_bc.1.0 row2_sum.1.1 tok_pe.0.5 row2_cp.1.0 tok_pe.0.6 coeff.0.5 "
-            "tok_pe.0.7 row2_rcp.1.1 coeff.0.6 row2_bc.1.1 coeff.0.7 row2_cp.1.1 c_quant.0.5 c_quant.0.6 "
-            "c_quant.0.7 o_pe.0.4 col2.1.0 o_pe.0.5 o_cp.0.4 o_pe.0.6 col2.1.1 o_cp.0.5 "
-            "o_pe.0.7 o_cp.0.6 col2_v.1.0 o_cp.0.7 col2.1.2 plan.1.0 col2_v.1.1 col2.1.3 "
-            "plan.1.1 tok_pe.1.0 tok_pe.1.1 col2_v.1.2 coeff.1.0 plan.1.2 tok_pe.1.2 col2_v.1.3 "
-            "coeff.1.1 tok_pe.1.3 c_quant.1.0 coeff.1.2 plan.1.3 tok_pe.1.4 c_quant.1.1 tok_pe.1.5 "
-            "coeff.1.3 o_pe.1.0 c_quant.1.2 coeff.1.4 tok_pe.1.6 o_cp.1.0 c_quant.1.3 coeff.1.5 "
-            "tok_pe.1.7 c_quant.1.4 coeff.1.6 o_pe.1.2 c_quant.1.5 coeff.1.7 o_cp.1.2 o_pe.1.1 "
-            "c_quant.1.6 o_cp.1.1 o_pe.1.4 c_quant.1.7 o_pe.1.3 o_cp.1.4 o_cp.1.3 o_pe.1.6 "
-            "o_pe.1.5 o_cp.1.6 o_cp.1.5 o_pe.1.7 o_cp.1.7 "
+            "xt_cp.1.1 row_v.0.0 mx1.0.2 widen.0.0 mx1.0.3 row_v.0.1 row_s.0.0 mx1.0.4 "
+            "row_v.0.2 widen.0.1 mx1.0.5 row_s.0.1 row_v.0.3 mx1.0.6 row_s.0.2 widen.0.2 "
+            "row_v.0.4 mx1.0.7 row_s.0.3 row_v.0.5 xt_pe.1.2 row_s.0.4 widen.0.3 row_v.0.6 "
+            "xt_pe.1.3 row_s.0.5 row_v.0.7 row_s.0.6 widen.0.4 qx.1.0 row_s.0.7 v_ilv.0.0 "
+            "mx1.1.0 xt_cp.1.2 v_ilv.0.1 widen.0.5 mx1.1.1 ln_a.0.0 row_v.1.0 xt_cp.1.3 "
+            "mx1.1.2 ln_b.0.0 row_v.1.1 v_ilv.0.3 widen.0.6 mx1.1.3 row_v.1.2 ln_s.0.1 "
+            "row_s.1.0 widen.0.7 ln_a.0.1 row_v.1.3 row_s.1.1 ln_b.0.1 row_s.1.2 qx.1.1 "
+            "v_ilv.0.2 ln_s.0.2 row_s.1.3 mx1.1.4 ln_a.0.2 v_ilv.0.4 mx1.1.5 v_ilv.0.7 "
+            "mx1.1.6 ln_b.0.2 row_v.1.4 mx1.1.7 ln_s.0.3 v_ilv.0.11 row_v.1.5 ln_a.0.3 "
+            "row_s.1.4 row_v.1.6 row_s.1.5 ln_b.0.3 row_v.1.7 row_s.1.6 ln_c.0.0 v_ilv.0.5 "
+            "col_pe.0.0 v_ilv.0.6 row_s.1.7 v_ilv.0.8 widen.1.0 col_pe.0.1 v_ilv.0.9 v_ilv.0.15 "
+            "col_max.0.0 col_pe.0.2 col_max.0.1 widen.1.1 col_pe.0.3 ln_a.1.0 col_max.0.2 col_min2.0.0 "
+            "ln_b.1.0 widen.1.2 v_ilv.0.10 col_exp.0.0 col_max.0.3 ln_s.1.1 col_exp.0.1 v_ilv.0.12 "
+            "col_pe.0.4 widen.1.3 col_min2.0.1 ln_a.1.1 v_ilv.0.13 col_exp.0.2 ln_b.1.1 col_pe.0.5 "
+            "col_add.0.0 v_ilv.0.14 ln_s.1.2 col_max.0.4 col_exp.0.3 widen.1.4 col_pe.0.6 col_max.0.5 "
+            "col_pe.0.7 col_rcp.0.0 col_max.0.6 widen.1.5 row2_scale.0.0 col_add.0.1 col_min2.0.2 ln_a.1.2 "
+            "col_max.0.7 col_exp.0.4 col_rcp.0.1 widen.1.6 ln_b.1.2 v_quant.0.0 row2_scale.0.1 widen.1.7 "
+            "col_min2.0.3 v_quant.0.1 ln_s.1.3 col_exp.0.5 col_exp.0.6 ln_a.1.3 v_ilv.1.0 col_add.0.2 "
+            "ln_b.1.3 v_ilv.1.1 col_exp.0.7 col_rcp.0.2 ln_c.1.0 v_ilv.1.2 col_pe.1.0 row2_scale.0.2 "
+            "v_ilv.1.4 col_add.0.3 v_ilv.1.5 col_pe.1.1 col_rcp.0.3 col_max.1.0 v_ilv.1.3 col_pe.1.2 "
+            "v_ilv.1.6 row2_scale.0.3 col_max.1.1 col_pe.1.3 col_max.1.2 v_ilv.1.7 col_min2.1.0 v_ilv.1.8 "
+            "col_max.1.3 col_exp.1.0 v_quant.1.0 col_exp.1.1 row2_pe.0.0 v_ilv.1.11 col_add.1.0 col_min2.1.1 "
+            "v_ilv.1.9 col_exp.1.2 col_rcp.1.0 v_ilv.1.10 row2_pe.0.1 v_ilv.1.12 row2_scale.1.0 row2_sum.0.0 "
+            "v_ilv.1.13 row2_rcp.0.0 col_exp.1.3 v_ilv.1.14 col_pe.1.4 row2_sum.0.1 v_ilv.1.15 row2_bc.0.0 "
+            "col_add.1.1 col_max.1.4 col_pe.1.5 row2_cp.0.0 row2_rcp.0.1 col_rcp.1.1 v_quant.1.1 row2_bc.0.1 "
+            "row2_scale.1.1 col_pe.1.6 col_max.1.5 col_pe.1.7 row2_cp.0.1 col_max.1.6 col_min2.1.2 col_max.1.7 "
+            "col_exp.1.4 col2.0.0 col_exp.1.5 col_min2.1.3 col_add.1.2 col2.0.1 col_exp.1.6 col_exp.1.7 "
+            "col2_v.0.0 col_rcp.1.2 col2.0.2 plan.0.0 col2_v.0.1 row2_scale.1.2 col_add.1.3 col2.0.3 "
+            "tok_pe.0.0 tok_pe.0.1 plan.0.1 col2_v.0.2 col_rcp.1.3 coeff.0.0 col2_v.0.3 coeff.0.1 "
+            "row2_scale.1.3 tok_pe.0.2 c_quant.0.0 c_quant.0.1 tok_pe.0.3 coeff.0.2 o_pe.0.0 plan.0.2 "
+            "coeff.0.3 row2_pe.1.0 c_quant.0.2 c_quant.0.3 o_cp.0.0 plan.0.3 row2_pe.1.1 row2_sum.1.0 "
+            "row2_rcp.1.0 tok_pe.0.4 row2_sum.1.1 tok_pe.0.5 coeff.0.4 tok_pe.0.6 tok_pe.0.7 row2_rcp.1.1 "
+            "coeff.0.5 row2_bc.1.0 coeff.0.6 row2_cp.1.0 row2_bc.1.1 c_quant.0.4 row2_cp.1.1 c_quant.0.5 "
+            "o_pe.0.1 c_quant.0.6 coeff.0.7 o_pe.0.2 o_cp.0.1 col2.1.0 o_pe.0.3 o_cp.0.2 "
+            "o_pe.0.4 o_cp.0.3 c_quant.0.7 col2.1.1 o_cp.0.4 col2_v.1.0 col2.1.2 plan.1.0 "
+            "o_pe.0.5 o_pe.0.6 col2_v.1.1 col2.1.3 o_cp.0.5 tok_pe.1.0 o_cp.0.6 tok_pe.1.1 "
+            "col2_v.1.2 plan.1.1 coeff.1.0 col2_v.1.3 coeff.1.1 o_pe.0.7 plan.1.2 c_quant.1.0 "
+            "c_quant.1.1 tok_pe.1.2 coeff.1.2 o_pe.1.0 o_cp.0.7 o_pe.1.1 c_quant.1.2 o_cp.1.0 "
+            "tok_pe.1.3 o_cp.1.1 coeff.1.3 plan.1.3 c_quant.1.3 tok_pe.1.4 coeff.1.4 o_pe.1.2 "
+            "c_quant.1.4 o_pe.1.3 o_cp.1.2 tok_pe.1.5 o_cp.1.3 tok_pe.1.6 coeff.1.5 coeff.1.6 "
+            "tok_pe.1.7 c_quant.1.5 coeff.1.7 o_pe.1.4 c_quant.1.6 c_quant.1.7 o_pe.1.5 o_cp.1.4 "
+            "o_pe.1.6 o_cp.1.5 o_pe.1.7 o_cp.1.6 o_cp.1.7 "
         )
         with tc.manual_schedule():
             for word in table.split(" "):

from contextlib import ExitStack

import concourse.mybir as mybir
from concourse.masks import make_identity

B, N, D, M, V = 2, 1024, 512, 512, 1024
FLOPS = 2 * B * N * D * M + 2 * B * N * M * V

P = 128
MMB, TLB = 4, 4
XTV = lambda b, j: b == 0 and j == 1
PLV = lambda b, k: False
OV = lambda b, j: b == 1 and j in (5, 7)
VIS = lambda b, i: i % 4 == 3
WG = lambda b, j: True
LN2 = 0.6931471805599453
F32 = mybir.dt.float32
BF16 = mybir.dt.bfloat16
I32 = mybir.dt.int32
U32 = mybir.dt.uint32
U8 = mybir.dt.uint8
FP8 = mybir.dt.float8_e4m3fn
FP8X4 = mybir.dt.float8_e4m3fn_x4
FP4X4 = mybir.dt.float4_e2m1fn_x4
ALU = mybir.AluOpType
ACT = mybir.ActivationFunctionType
X = mybir.AxisListType.X


def tile_sinkhornbalancedslotdispatch_d2p_kernel(tc, x, phi_words, phi_scales, w, v_bytes, v_scale, out):
    nc = tc.nc
    with ExitStack() as ctx:
        keep = ctx.enter_context(tc.tile_pool(name="keep", bufs=1))
        work = ctx.enter_context(tc.tile_pool(name="work", bufs=2))
        psum = ctx.enter_context(tc.psum_pool(name="psum", bufs=1))

        ident = keep.tile([P, P], F32, name="ident")
        make_identity(nc, ident[:])

        phi_w = keep.tile([P, 2 * M], U8, name="phi_w", align_bytes=64)
        phi_s = keep.tile([P, M], U8, name="phi_s", align_bytes=64)
        nc.vector.memset(phi_s[:].bitcast(I32), 0)
        for q in range(4):
            nc.scalar.dma_start(out=phi_s[32 * q : 32 * q + 4, :].bitcast(I32), in_=phi_scales[0, 4 * q : 4 * q + 4, :].bitcast(I32))
        nc.scalar.dma_start(out=phi_w[:].bitcast(I32), in_=phi_words[0].bitcast(I32))

        x_sb = [[keep.tile([P, 4, D], BF16, name=f"x_{b}_{g}") for g in range(2)] for b in range(B)]
        vb = [[keep.tile([P, 4, V], U8, name=f"vbytes_{b}_{g}") for g in range(2)] for b in range(B)]

        def load_x(b, g):
            nc.sync.dma_start(out=x_sb[b][g][:], in_=x[b].rearrange("(g p t) k -> g p t k", p=P, t=4)[g])

        def load_v(b, g):
            nc.sync.dma_start(out=vb[b][g][:], in_=v_bytes[b].rearrange("(g p t) j -> g p t j", p=P, t=4)[g])

        load_x(0, 0)
        load_x(0, 1)
        load_v(0, 0)
        load_x(1, 0)
        load_x(1, 1)
        load_v(0, 1)
        load_v(1, 0)
        load_v(1, 1)

        w_bf = keep.tile([P, 2, 4], BF16, name="w_bf")
        nc.gpsimd.dma_start(out=w_bf[:], in_=w.rearrange("(g p t) -> p g t", p=P, t=4))
        vs = keep.tile([P, 4, 8], F32, name="vs")
        vs_src = v_scale.rearrange("b i j -> (b i) j").rearrange("(c q) j -> q c j", q=4)
        for q in range(4):
            nc.gpsimd.dma_start(out=vs[32 * q : 32 * q + 32], in_=vs_src[q].partition_broadcast(32))

        w32 = keep.tile([P, 8], F32, name="w32")

        xc = [[keep.tile([P, 512], U32, name=f"xc_{b}_{g}", align_bytes=64) for g in range(2)] for b in range(B)]
        xs = [[keep.tile([P, 512], U8, name=f"xs_{b}_{g}", align_bytes=64) for g in range(2)] for b in range(B)]
        cq = [[keep.tile([P, 512], U32, name=f"cq_{b}_{g}", align_bytes=64) for g in range(2)] for b in range(B)]
        cs = [[keep.tile([P, 512], U8, name=f"cs_{b}_{g}", align_bytes=64) for g in range(2)] for b in range(B)]
        vq = [[keep.tile([P, V], U32, name=f"vq_{b}_{g}", align_bytes=64) for g in range(2)] for b in range(B)]
        vqs = [[keep.tile([P, V], U8, name=f"vqs_{b}_{g}", align_bytes=64) for g in range(2)] for b in range(B)]
        nl = [keep.tile([P, 8, M], F32, name=f"nl_{b}") for b in range(B)]
        et = [keep.tile([P, 4, N], F32, name=f"et_{b}") for b in range(B)]
        na = [keep.tile([P, 8], F32, name=f"na_{b}") for b in range(B)]
        r1 = [keep.tile([P, 8], F32, name=f"r1_{b}") for b in range(B)]
        lnr = [keep.tile([P, 8], F32, name=f"lnr_{b}") for b in range(B)]
        lnt = [keep.tile([P, 8], F32, name=f"lnt_{b}") for b in range(B)]
        lse = [keep.tile([P, 8], F32, name=f"lse_{b}") for b in range(B)]
        nb2 = [keep.tile([P, 4, 2], F32, name=f"nb2_{b}") for b in range(B)]
        nb = [keep.tile([P, 4], F32, name=f"nb_{b}") for b in range(B)]
        s1 = [keep.tile([P, 4, 2], F32, name=f"s1_{b}") for b in range(B)]
        s1t = [keep.tile([P, 4], F32, name=f"s1t_{b}") for b in range(B)]
        v1 = [keep.tile([P, 4], F32, name=f"v1_{b}") for b in range(B)]
        s2 = [keep.tile([P, 4], F32, name=f"s2_{b}") for b in range(B)]
        usb = [keep.tile([P, N], F32, name=f"usb_{b}") for b in range(B)]
        r2 = [keep.tile([P, 8], F32, name=f"r2_{b}") for b in range(B)]
        u2 = [keep.tile([P, 8], F32, name=f"u2_{b}") for b in range(B)]
        v2 = [keep.tile([P, 4], F32, name=f"v2_{b}") for b in range(B)]

        xt_ps = {}
        o_ps = {}
        xg = {}
        wide = {}
        vg = {}
        cc = {}
        cgs = {}
        slot_ps = {}
        r2_ps = {}
        l_ps = {}

        def xt_pe(b, j):
            g, h = divmod(j, 2)
            ps = psum.tile([P, 2, 2, P], F32, name="xt_ps", tag="mm", bufs=MMB)
            words = x_sb[b][g][:].bitcast(F32)
            for k in range(2):
                for e in range(2):
                    nc.tensor.transpose(ps[:, k, e, :], words[:, 2 * h + k, e:256:2], ident[:])
            xt_ps[b, j] = ps

        def xt_cp(b, j):
            g, h = divmod(j, 2)
            if (b, g) not in xg:
                xg[b, g] = work.tile([P, 512, 4], BF16, name="xg", tag="xg", bufs=2, align_bytes=64)
            dst = xg[b, g][:].bitcast(F32)[:, 256 * h : 256 * h + 256, :].rearrange("p (k r) e -> p k r e", k=2)
            src = xt_ps[b, j][:].rearrange("p k e r -> p k r e")
            if XTV(b, j):
                nc.vector.tensor_copy(out=dst, in_=src)
            else:
                nc.scalar.copy(out=dst, in_=src)

        def qx(b, g):
            nc.vector.quantize_mx(out=xc[b][g][:].bitcast(FP8X4), scales=xs[b][g][:], in_=xg[b, g][:].rearrange("p r k -> p (r k)"))

        def mx1(b, i):
            g, t = i // 4, i % 4
            ps = psum.tile([P, M], F32, name="l_ps", tag="mm", bufs=MMB)
            nc.tensor.matmul_mx(
                out=ps[:],
                lhsT=xc[b][g][:, P * t : P * t + P].bitcast(FP8X4),
                lhsT_scale=xs[b][g][:, P * t : P * t + P],
                rhs=phi_w[:].bitcast(FP4X4),
                rhs_scale=phi_s[:],
                start=True,
                stop=True,
            )
            l_ps[b, i] = ps

        def row_v(b, i):
            nc.vector.tensor_scalar(out=nl[b][:, i, :], in0=l_ps[b, i][:], scalar1=-1.0, scalar2=None, op0=ALU.mult, op1=ALU.min, accum_out=na[b][:, i : i + 1])

        def row_s(b, i):
            junk = work.tile([P, M], BF16, name="junk", tag="junk", bufs=2)
            nc.scalar.activation(out=junk[:], in_=nl[b][:, i, :], func=ACT.Exp, scale=-1.0, bias=na[b][:, i : i + 1], accum_out=r1[b][:, i : i + 1])

        def ln_a(b, n):
            if n == 0:
                nc.vector.tensor_copy(out=lnt[b][:], in_=r1[b][:].bitcast(I32))
            else:
                nc.vector.tensor_tensor(out=lnt[b][:], in0=lnt[b][:], in1=r1[b][:], op=ALU.mult)

        def ln_b(b, n):
            y, f = lnr[b][:], lnt[b][:]
            if n == 0:
                nc.vector.tensor_scalar(out=y, in0=f, scalar1=LN2 / 2**23, scalar2=-126.957 * LN2, op0=ALU.mult, op1=ALU.add)
            else:
                nc.vector.scalar_tensor_tensor(out=y, in0=f, scalar=-1.0, in1=y, op0=ALU.add, op1=ALU.add)

        def ln_c(b, n):
            nc.vector.tensor_tensor(out=lse[b][:], in0=lnr[b][:], in1=na[b][:], op=ALU.subtract)

        def ln_s(b, n):
            nc.scalar.activation(out=lnt[b][:], in_=lnr[b][:], func=ACT.Exp, scale=-1.0)

        def col_pe(b, j):
            k, g = divmod(j, 2)
            ps = psum.tile([P, 4, P], F32, name="t_ps", tag="tl", bufs=TLB)
            for t in range(4):
                i = 4 * g + t
                nc.tensor.matmul(ps[:, t, :], lhsT=nl[b][:, i, P * k : P * k + P], rhs=ident[:], is_transpose=True, start=True, stop=False)
                nc.tensor.matmul(ps[:, t, :], lhsT=lse[b][:, i : i + 1].to_broadcast([P, P]), rhs=ident[:], is_transpose=True, start=False, stop=True)
            slot_ps[b, k, g] = ps

        def col_max(b, j):
            k, g = divmod(j, 2)
            nc.vector.tensor_reduce(out=nb2[b][:, k, g : g + 1], in_=slot_ps[b, k, g][:].rearrange("p t r -> p (t r)"), axis=X, op=ALU.min)

        def col_min2(b, k):
            nc.vector.tensor_tensor(out=nb[b][:, k : k + 1], in0=nb2[b][:, k, 0:1], in1=nb2[b][:, k, 1:2], op=ALU.min)

        def col_exp(b, j):
            k, g = divmod(j, 2)
            nc.scalar.activation(
                out=et[b][:, k, 512 * g : 512 * g + 512],
                in_=slot_ps[b, k, g][:].rearrange("p t r -> p (t r)"),
                func=ACT.Exp,
                scale=-1.0,
                bias=nb[b][:, k : k + 1],
                accum_out=s1[b][:, k, g : g + 1],
            )

        def col_add(b, k):
            nc.vector.tensor_tensor(out=s1t[b][:, k : k + 1], in0=s1[b][:, k, 0:1], in1=s1[b][:, k, 1:2], op=ALU.add)

        def col_rcp(b, k):
            nc.vector.reciprocal(out=v1[b][:, k : k + 1], in_=s1t[b][:, k : k + 1])

        def row2_scale(b, k):
            nc.scalar.activation(out=et[b][:, k, :], in_=et[b][:, k, :], func=ACT.Copy, scale=v1[b][:, k : k + 1])

        def row2_pe(b, g):
            ps = psum.tile([P, 4, P], F32, name="r2_ps", tag="tl", bufs=TLB)
            for t in range(4):
                i = 4 * g + t
                for k in range(4):
                    nc.tensor.matmul(ps[:, t, :], lhsT=et[b][:, k, P * i : P * i + P], rhs=ident[:], is_transpose=True, start=(k == 0), stop=(k == 3))
            r2_ps[b, g] = ps

        def row2_sum(b, g):
            nc.vector.tensor_reduce(out=r2[b][:, 4 * g : 4 * g + 4], in_=r2_ps[b, g][:], axis=X, op=ALU.add)

        def row2_rcp(b, g):
            nc.vector.reciprocal(out=u2[b][:, 4 * g : 4 * g + 4], in_=r2[b][:, 4 * g : 4 * g + 4])

        ubc = {}

        def row2_bc(b, g):
            ps = psum.tile([P, 4, P], F32, name="u_ps", tag="mm", bufs=MMB)
            for t in range(4):
                i = 4 * g + t
                nc.tensor.matmul(ps[:, t, :], lhsT=u2[b][:, i : i + 1].to_broadcast([P, P]), rhs=ident[:], is_transpose=True, start=True, stop=True)
            ubc[b, g] = ps

        def row2_cp(b, g):
            nc.scalar.copy(out=usb[b][:, 512 * g : 512 * g + 512], in_=ubc[b, g][:].rearrange("p t r -> p (t r)"))

        def col2(b, k):
            e = et[b][:, k, :]
            nc.vector.scalar_tensor_tensor(out=e, in0=e, scalar=1.0, in1=usb[b][:], op0=ALU.mult, op1=ALU.mult, accum_out=s2[b][:, k : k + 1])

        def col2_v(b, k):
            nc.vector.reciprocal(out=v2[b][:, k : k + 1], in_=s2[b][:, k : k + 1])

        def plan(b, k):
            e = et[b][:, k, :]
            if PLV(b, k):
                nc.vector.tensor_scalar(out=e, in0=e, scalar1=v2[b][:, k : k + 1], scalar2=-1.0 / N, op0=ALU.mult, op1=ALU.add)
            else:
                nc.scalar.activation(out=e, in_=e, func=ACT.Identity, scale=v2[b][:, k : k + 1], bias=-1.0 / N)

        tok_ps = {}
        cg = {}

        def tok_pe(b, j):
            k, g = divmod(j, 2)
            ps = psum.tile([P, 4, P], F32, name="tok_ps", tag="mm", bufs=MMB)
            for t in range(4):
                i = 4 * g + t
                nc.tensor.transpose(ps[:, t, :], et[b][:, k, P * i : P * i + P], ident[:])
            tok_ps[b, j] = ps

        def coeff(b, j):
            k, g = divmod(j, 2)
            cg[b, j] = work.tile([P, P, 4], BF16, name="cg", tag="cg", bufs=3, align_bytes=64)
            nc.vector.tensor_tensor(
                out=cg[b, j][:],
                in0=tok_ps[b, j][:].rearrange("p t m -> p m t"),
                in1=w32[:, 4 * g : 4 * g + 4].unsqueeze(1).to_broadcast([P, P, 4]),
                op=ALU.mult,
            )

        def c_quant(b, j):
            k, g = divmod(j, 2)
            nc.vector.quantize_mx(out=cq[b][g][:, P * k : P * k + P].bitcast(FP8X4), scales=cs[b][g][:, P * k : P * k + P], in_=cg[b, j][:].rearrange("p m t -> p (m t)"))

        def widen(b, j):
            g, t = divmod(j, 4)
            if (b, g) not in wide:
                wide[b, g] = work.tile([P, 4, V], BF16, name="wide", tag="wide", bufs=2)
            src = vb[b][g][:, t, :].bitcast(FP8)
            if WG(b, j):
                nc.gpsimd.tensor_copy(out=wide[b, g][:, t, :], in_=src)
            else:
                nc.scalar.copy(out=wide[b, g][:, t, :], in_=src)

        def v_ilv(b, i):
            g, j = divmod(i, 8)
            if (b, g) not in vg:
                vg[b, g] = work.tile([P, V, 4], BF16, name="vg", tag="vg", bufs=2, align_bytes=64)
            dst = vg[b, g][:, P * j : P * j + P, :]
            src = wide[b, g][:, :, P * j : P * j + P].rearrange("p t j -> p j t")
            if VIS(b, i):
                nc.scalar.activation(out=dst, in_=src, func=ACT.Copy, scale=vs[:, 2 * b + g, j : j + 1])
            else:
                nc.vector.tensor_scalar(out=dst, in0=src, scalar1=vs[:, 2 * b + g, j : j + 1], scalar2=None, op0=ALU.mult)

        def v_quant(b, g):
            nc.vector.quantize_mx(out=vq[b][g][:].bitcast(FP8X4), scales=vqs[b][g][:], in_=vg[b, g][:].rearrange("p j t -> p (j t)"))

        def o_pe(b, j):
            mb, jh = divmod(j, 2)
            ps = psum.tile([P, 512], F32, name="o_ps", tag="mm", bufs=MMB)
            for g in range(2):
                nc.tensor.matmul_mx(
                    out=ps[:],
                    lhsT=cq[b][g][:, P * mb : P * mb + P].bitcast(FP8X4),
                    lhsT_scale=cs[b][g][:, P * mb : P * mb + P],
                    rhs=vq[b][g][:, 512 * jh : 512 * jh + 512].bitcast(FP8X4),
                    rhs_scale=vqs[b][g][:, 512 * jh : 512 * jh + 512],
                    start=(g == 0),
                    stop=(g == 1),
                )
            o_ps[b, j] = ps

        def o_cp(b, j):
            mb, jh = divmod(j, 2)
            ot = work.tile([P, 512], F32, name="ot", tag="ot", bufs=8)
            if OV(b, j):
                nc.vector.tensor_scalar(out=ot[:], in0=o_ps[b, j][:], scalar1=1.0 / 32.0, scalar2=None, op0=ALU.mult)
            else:
                nc.scalar.activation(out=ot[:], in_=o_ps[b, j][:], func=ACT.Copy, scale=1.0 / 32.0)
            nc.sync.dma_start(out=out[b, P * mb : P * mb + P, 512 * jh : 512 * jh + 512], in_=ot[:])

        def prep_w(b, j):
            nc.vector.tensor_scalar(out=w32[:], in0=w_bf[:].rearrange("p g t -> p (g t)"), scalar1=float(N), scalar2=None, op0=ALU.mult)

        byname = {"xt_pe": xt_pe, "xt_cp": xt_cp, "qx": qx, "mx1": mx1, "row_v": row_v, "row_s": row_s, "ln_a": ln_a, "ln_b": ln_b, "ln_s": ln_s, "ln_c": ln_c, "prep_w": prep_w, "col_pe": col_pe, "col_max": col_max, "col_min2": col_min2, "col_exp": col_exp, "col_add": col_add, "col_rcp": col_rcp, "row2_scale": row2_scale, "row2_pe": row2_pe, "row2_sum": row2_sum, "row2_rcp": row2_rcp, "row2_bc": row2_bc, "row2_cp": row2_cp, "col2": col2, "col2_v": col2_v, "plan": plan, "tok_pe": tok_pe, "coeff": coeff, "c_quant": c_quant, "widen": widen, "v_ilv": v_ilv, "v_quant": v_quant, "o_pe": o_pe, "o_cp": o_cp}
        table = (
            "xt_pe.0.0 xt_pe.0.1 xt_cp.0.0 xt_pe.0.2 xt_cp.0.1 xt_pe.0.3 xt_cp.0.2 qx.0.0 "
            "xt_pe.1.0 xt_cp.0.3 prep_w.0.0 xt_pe.1.1 xt_cp.1.0 qx.0.1 mx1.0.0 mx1.0.1 "
            "xt_cp.1.1 row_v.0.0 mx1.0.2 widen.0.0 mx1.0.3 row_v.0.1 row_s.0.0 mx1.0.4 "
            "row_v.0.2 widen.0.1 mx1.0.5 row_s.0.1 row_v.0.3 mx1.0.6 row_s.0.2 widen.0.2 "
            "row_v.0.4 mx1.0.7 row_s.0.3 row_v.0.5 xt_pe.1.2 row_s.0.4 widen.0.3 row_v.0.6 "
            "xt_pe.1.3 row_s.0.5 row_v.0.7 row_s.0.6 widen.0.4 qx.1.0 row_s.0.7 v_ilv.0.0 "
            "mx1.1.0 xt_cp.1.2 v_ilv.0.1 widen.0.5 mx1.1.1 ln_a.0.0 row_v.1.0 xt_cp.1.3 "
            "mx1.1.2 ln_b.0.0 row_v.1.1 v_ilv.0.3 widen.0.6 mx1.1.3 row_v.1.2 ln_s.0.1 "
            "row_s.1.0 widen.0.7 ln_a.0.1 row_v.1.3 row_s.1.1 ln_b.0.1 row_s.1.2 qx.1.1 "
            "v_ilv.0.2 ln_s.0.2 row_s.1.3 mx1.1.4 ln_a.0.2 v_ilv.0.4 mx1.1.5 v_ilv.0.7 "
            "mx1.1.6 ln_b.0.2 row_v.1.4 mx1.1.7 ln_s.0.3 v_ilv.0.11 row_v.1.5 ln_a.0.3 "
            "row_s.1.4 row_v.1.6 row_s.1.5 ln_b.0.3 row_v.1.7 row_s.1.6 ln_c.0.0 v_ilv.0.5 "
            "col_pe.0.0 v_ilv.0.6 row_s.1.7 v_ilv.0.8 widen.1.0 col_pe.0.1 v_ilv.0.9 v_ilv.0.15 "
            "col_max.0.0 col_pe.0.2 col_max.0.1 widen.1.1 col_pe.0.3 ln_a.1.0 col_max.0.2 col_min2.0.0 "
            "ln_b.1.0 widen.1.2 v_ilv.0.10 col_exp.0.0 col_max.0.3 ln_s.1.1 col_exp.0.1 v_ilv.0.12 "
            "col_pe.0.4 widen.1.3 col_min2.0.1 ln_a.1.1 v_ilv.0.13 col_exp.0.2 ln_b.1.1 col_pe.0.5 "
            "col_add.0.0 v_ilv.0.14 ln_s.1.2 col_max.0.4 col_exp.0.3 widen.1.4 col_pe.0.6 col_max.0.5 "
            "col_pe.0.7 col_rcp.0.0 col_max.0.6 widen.1.5 row2_scale.0.0 col_add.0.1 col_min2.0.2 ln_a.1.2 "
            "col_max.0.7 col_exp.0.4 col_rcp.0.1 widen.1.6 ln_b.1.2 v_quant.0.0 row2_scale.0.1 widen.1.7 "
            "col_min2.0.3 v_quant.0.1 ln_s.1.3 col_exp.0.5 col_exp.0.6 ln_a.1.3 v_ilv.1.0 col_add.0.2 "
            "ln_b.1.3 v_ilv.1.1 col_exp.0.7 col_rcp.0.2 ln_c.1.0 v_ilv.1.2 col_pe.1.0 row2_scale.0.2 "
            "v_ilv.1.4 col_add.0.3 v_ilv.1.5 col_pe.1.1 col_rcp.0.3 col_max.1.0 v_ilv.1.3 col_pe.1.2 "
            "v_ilv.1.6 row2_scale.0.3 col_max.1.1 col_pe.1.3 col_max.1.2 v_ilv.1.7 col_min2.1.0 v_ilv.1.8 "
            "col_max.1.3 col_exp.1.0 v_quant.1.0 col_exp.1.1 row2_pe.0.0 v_ilv.1.11 col_add.1.0 col_min2.1.1 "
            "v_ilv.1.9 col_exp.1.2 col_rcp.1.0 v_ilv.1.10 row2_pe.0.1 v_ilv.1.12 row2_scale.1.0 row2_sum.0.0 "
            "v_ilv.1.13 row2_rcp.0.0 col_exp.1.3 v_ilv.1.14 col_pe.1.4 row2_sum.0.1 v_ilv.1.15 row2_bc.0.0 "
            "col_add.1.1 col_max.1.4 col_pe.1.5 row2_cp.0.0 row2_rcp.0.1 col_rcp.1.1 v_quant.1.1 row2_bc.0.1 "
            "row2_scale.1.1 col_pe.1.6 col_max.1.5 col_pe.1.7 row2_cp.0.1 col_max.1.6 col_min2.1.2 col_max.1.7 "
            "col_exp.1.4 col2.0.0 col_exp.1.5 col_min2.1.3 col_add.1.2 col2.0.1 col_exp.1.6 col_exp.1.7 "
            "col2_v.0.0 col_rcp.1.2 col2.0.2 plan.0.0 col2_v.0.1 row2_scale.1.2 col_add.1.3 col2.0.3 "
            "tok_pe.0.0 tok_pe.0.1 plan.0.1 col2_v.0.2 col_rcp.1.3 coeff.0.0 col2_v.0.3 coeff.0.1 "
            "row2_scale.1.3 tok_pe.0.2 c_quant.0.0 c_quant.0.1 tok_pe.0.3 coeff.0.2 o_pe.0.0 plan.0.2 "
            "coeff.0.3 row2_pe.1.0 c_quant.0.2 c_quant.0.3 o_cp.0.0 plan.0.3 row2_pe.1.1 row2_sum.1.0 "
            "row2_rcp.1.0 tok_pe.0.4 row2_sum.1.1 tok_pe.0.5 coeff.0.4 tok_pe.0.6 tok_pe.0.7 row2_rcp.1.1 "
            "coeff.0.5 row2_bc.1.0 coeff.0.6 row2_cp.1.0 row2_bc.1.1 c_quant.0.4 row2_cp.1.1 c_quant.0.5 "
            "o_pe.0.1 c_quant.0.6 coeff.0.7 o_pe.0.2 o_cp.0.1 col2.1.0 o_pe.0.3 o_cp.0.2 "
            "o_pe.0.4 o_cp.0.3 c_quant.0.7 col2.1.1 o_cp.0.4 col2_v.1.0 col2.1.2 plan.1.0 "
            "o_pe.0.5 o_pe.0.6 col2_v.1.1 col2.1.3 o_cp.0.5 tok_pe.1.0 o_cp.0.6 tok_pe.1.1 "
            "col2_v.1.2 plan.1.1 coeff.1.0 col2_v.1.3 coeff.1.1 o_pe.0.7 plan.1.2 c_quant.1.0 "
            "c_quant.1.1 tok_pe.1.2 coeff.1.2 o_pe.1.0 o_cp.0.7 o_pe.1.1 c_quant.1.2 o_cp.1.0 "
            "tok_pe.1.3 o_cp.1.1 coeff.1.3 plan.1.3 c_quant.1.3 tok_pe.1.4 coeff.1.4 o_pe.1.2 "
            "c_quant.1.4 o_pe.1.3 o_cp.1.2 tok_pe.1.5 o_cp.1.3 tok_pe.1.6 coeff.1.5 coeff.1.6 "
            "tok_pe.1.7 c_quant.1.5 coeff.1.7 o_pe.1.4 c_quant.1.6 c_quant.1.7 o_pe.1.5 o_cp.1.4 "
            "o_pe.1.6 o_cp.1.5 o_pe.1.7 o_cp.1.6 o_cp.1.7 "
        )
        with tc.manual_schedule():
            for word in table.split(" "):
                if word:
                    name, b, j = word.split(".")
                    byname[name](int(b), int(j))
